import numpy as np
import ml_dtypes


def mxq(x, axis, fmt="e4m3"):
    dtype, down = {"e4m3": (ml_dtypes.float8_e4m3fn, 7), "e5m2": (ml_dtypes.float8_e5m2, 14)}[fmt]
    v = np.moveaxis(np.asarray(x, np.float32).astype(ml_dtypes.bfloat16).astype(np.float64), axis, -1)
    blocks = v.reshape(v.shape[:-1] + (-1, 32))
    amax = np.abs(blocks).max(-1, keepdims=True)
    byte = np.maximum(np.where(amax > 0, np.frexp(amax)[1] - 1 + 127, 0) - down, 1)
    scale = np.exp2(byte - 127.0)
    codes = (blocks / scale).astype(np.float32).astype(dtype).astype(np.float64)
    return np.moveaxis((codes * scale).reshape(v.shape), -1, axis)


WIDE = False


def mx_kscale(k):
    if not WIDE:
        return np.ones(k)
    levels = np.array([30, -30])
    if k % 512:
        return np.exp2(np.random.permutation(np.resize(levels, k // 32))).repeat(32)
    a = np.empty((k // 512, 16))
    for p in range(k // 512):
        a[p, :8] = np.random.permutation(np.resize(levels, 8))
        for g in range(8):
            far = levels[np.abs(levels - a[p, g]) >= 10]
            a[p, g + 8] = far[np.random.randint(len(far))]
    return np.exp2(a.ravel()).repeat(32)


def f64(x):
    return np.asarray(x).astype(np.float64)


def striped(idx):
    return np.tile(np.asarray(idx).reshape(-1, 16).T, (8, 1)).astype(np.uint16)


def unstriped(offs):
    return offs[:16].T.reshape(-1).astype(np.int64)


E2M1 = np.array([0.0, 0.5, 1.0, 1.5, 2.0, 3.0, 4.0, 6.0, -0.0, -0.5, -1.0, -1.5, -2.0, -3.0, -4.0, -6.0])


def pack_weight(w, fmt):
    k, n = w.shape
    w = f64(np.asarray(w, np.float32).astype(ml_dtypes.bfloat16)).reshape(k // 32, 32, n)
    amax = np.abs(w).max(1)
    if fmt in ("e4m3", "e5m2"):
        byte = np.frexp(amax)[1] - 1 + 127 - (7 if fmt == "e4m3" else 14)
    else:
        mant, ex = np.frexp(amax / 6.0)
        byte = np.where(mant > 0.5, ex, ex - 1) + 127
    byte = np.clip(np.where(amax > 0, byte, 1), 1, 254)
    scaled = (w * np.exp2(127.0 - byte)[:, None, :]).reshape(k, n).astype(np.float32)
    by_word = np.ascontiguousarray(scaled.reshape(k // 512, 128, 4, n).transpose(0, 1, 3, 2))
    if fmt in ("e4m3", "e5m2"):
        words = by_word.astype(ml_dtypes.float8_e4m3fn if fmt == "e4m3" else ml_dtypes.float8_e5m2).view(np.uint8)
    else:
        c = by_word.astype(ml_dtypes.float4_e2m1fn).view(np.uint8) & 0xF
        words = (c[..., 0::2] | (c[..., 1::2] << 4)).reshape(k // 512, 128, 2 * n)
    return np.ascontiguousarray(words), np.ascontiguousarray(byte.astype(np.uint8).reshape(k // 512, 16, n))


def unpack_weight(words, scales, fmt):
    g, _, n = scales.shape
    words = np.ascontiguousarray(words).reshape(g, 128, n, -1)
    if fmt in ("e4m3", "e5m2"):
        vals = words.view(ml_dtypes.float8_e4m3fn if fmt == "e4m3" else ml_dtypes.float8_e5m2).astype(np.float64)
    else:
        nib = np.empty((g, 128, n, 4), np.uint8)
        nib[..., 0::2] = words & 0xF
        nib[..., 1::2] = words >> 4
        vals = E2M1[nib]
    vals = vals * np.repeat(np.exp2(scales.astype(np.float64) - 127.0), 8, axis=1)[..., None]
    return vals.transpose(0, 1, 3, 2).reshape(g * 512, n)


def sigmoid(v):
    return 1.0 / (1.0 + np.exp(-v))


K, F, T, Z, J, R, C, O, N, L, E = 512, 512, 1024, 1024, 256, 512, 512, 256, 256, 512, 1024


def setup_inputs():
    n = np.random.standard_normal
    idx = np.random.permutation(T)[:J]
    idx2 = np.random.permutation(Z)[:J]
    idx3 = np.random.permutation(C)[:J]
    idx4 = np.random.permutation(C)[:J]
    idx5 = np.random.permutation(C)[:O]
    idx6 = np.random.permutation(E)[:O]
    fk = mx_kscale(K)
    fr = mx_kscale(R)
    ff = mx_kscale(F)
    fl = mx_kscale(L)
    xtp = pack_weight(n((K, T)) / fk[:, None], "e2m1")
    wp = pack_weight(n((K, R)) * 1 / np.sqrt(K) * fk[:, None] * fr, "e5m2")
    xop = pack_weight(n((F, Z)) / ff[:, None], "e5m2")
    w2p = pack_weight(n((F, R)) * 1 / np.sqrt(F) * ff[:, None] * fr, "e4m3")
    wbp = pack_weight(n((R, N)) * 1 / np.sqrt(R) / fr[:, None], "e4m3")
    sxp = pack_weight(n((L, O)) / fl[:, None], "e5m2")
    wsp = pack_weight(n((L, N)) * 1 / np.sqrt(L) * fl[:, None], "e4m3")
    return {
        "xt_words": xtp[0],
        "xt_scales": xtp[1],
        "w_words": wp[0],
        "w_scales": wp[1],
        "xo_words": xop[0],
        "xo_scales": xop[1],
        "w2_words": w2p[0],
        "w2_scales": w2p[1],
        "wb_words": wbp[0],
        "wb_scales": wbp[1],
        "sx_words": sxp[0],
        "sx_scales": sxp[1],
        "ws_words": wsp[0],
        "ws_scales": wsp[1],
        "tz": (n((N, E))).astype(np.float32),
        "so": (np.random.uniform(0.6, 1.6, (N, 1))).astype(np.float32),
        "bo": (np.random.uniform(-1.0, 1.0, (N, 1))).astype(np.float32),
        "offs": striped(idx),
        "offs2": striped(idx2),
        "offs3": striped(idx3),
        "offs4": striped(idx4),
        "offs5": striped(idx5),
        "offs6": striped(idx6),
    }


def reference(xt_words, xt_scales, w_words, w_scales, xo_words, xo_scales, w2_words, w2_scales, wb_words, wb_scales, sx_words, sx_scales, ws_words, ws_scales, tz, so, bo, offs, offs2, offs3, offs4, offs5, offs6):
    idx = unstriped(offs)
    idx2 = unstriped(offs2)
    idx3 = unstriped(offs3)
    idx4 = unstriped(offs4)
    idx5 = unstriped(offs5)
    idx6 = unstriped(offs6)
    xtu = unpack_weight(xt_words, xt_scales, "e2m1")
    wu = unpack_weight(w_words, w_scales, "e5m2")
    xou = unpack_weight(xo_words, xo_scales, "e5m2")
    w2u = unpack_weight(w2_words, w2_scales, "e4m3")
    wbu = unpack_weight(wb_words, wb_scales, "e4m3")
    sxu = unpack_weight(sx_words, sx_scales, "e5m2")
    wsu = unpack_weight(ws_words, ws_scales, "e4m3")
    xtidxg = xtu[:, idx]
    a = wu.T @ xtidxg
    xoidx2g = xou[:, idx2]
    b = w2u.T @ xoidx2g
    pw = np.zeros((R, C))
    pw[:, idx3] = a
    pv = np.zeros((R, C))
    pv[:, idx4] = b
    pg = pw + pv
    hid = pg[:, idx5]
    hidq = mxq(hid, 0, "e5m2")
    p = wbu.T @ hidq + wsu.T @ sxu
    y = p * sigmoid(f64(tz)[:, idx6] * f64(so) + f64(bo))
    return y

@@ -1,0 +1,201 @@
+from contextlib import ExitStack
+
+import concourse.mybir as mybir
+
+K, F, T, Z, J, R, C, O, N, L, E = 512, 512, 1024, 1024, 256, 512, 512, 256, 256, 512, 1024
+FLOPS = 2 * (K * R * J + F * R * J + R * N * O + L * N * O)
+
+F32 = mybir.dt.float32
+BF16 = mybir.dt.bfloat16
+I32 = mybir.dt.int32
+U32 = mybir.dt.uint32
+U16 = mybir.dt.uint16
+U8 = mybir.dt.uint8
+E4M3 = mybir.dt.float8_e4m3fn_x4
+E5M2 = mybir.dt.float8_e5m2_x4
+E2M1 = mybir.dt.float4_e2m1fn_x4
+ACT = mybir.ActivationFunctionType
+ALU = mybir.AluOpType
+
+P = 128
+PACK = 4
+HALVES = N // P
+
+
+def tile_list_twotab_shared_skip_finalgate_kernel(
+    tc, xt_words, xt_scales, w_words, w_scales, xo_words, xo_scales, w2_words, w2_scales,
+    wb_words, wb_scales, sx_words, sx_scales, ws_words, ws_scales, tz, so, bo,
+    offs, offs2, offs3, offs4, offs5, offs6, out,
+):
+    nc = tc.nc
+    with ExitStack() as ctx:
+        sb = ctx.enter_context(tc.tile_pool(name="sb", bufs=1))
+        ps = ctx.enter_context(tc.psum_pool(name="ps", bufs=1))
+
+        def new(name, width, dtype, tag=""):
+            return sb.tile([P, width], dtype, name=name, tag=tag or name, align_bytes=64)
+
+        def load_list(name, src):
+            dst = sb.tile([P, J // 16], U16, name=name)
+            nc.sync.dma_start(dst[:], src)
+            return dst
+
+        def load_words(queue, name, src, width, dtype, tag=""):
+            dst = new(name, width, dtype, tag)
+            queue.dma_start(dst[:].bitcast(I32), src.bitcast(I32))
+            return dst
+
+        def zeroed_plane(engine, name, width):
+            plane = new(name, width, U8)
+            engine.memset(plane[:].bitcast(I32), 0)
+            return plane
+
+        def load_plane(queue, plane, src):
+            for q in range(4):
+                queue.dma_start(plane[32 * q : 32 * q + 4, :].bitcast(I32), src[0, 4 * q : 4 * q + 4, :].bitcast(I32))
+
+        def fp8_words(src):
+            return src[0].rearrange("p c r -> p (c r)")
+
+        def deal(copy, name, src, dtype, tag=""):
+            dst = new(name, R, dtype, tag)
+            copy(dst[:].rearrange("p (t m) -> p m t", t=PACK), src[:].rearrange("p (m t) -> p m t", t=PACK))
+            return dst
+
+        def gather(name, table, offsets, dtype, tag=""):
+            dst = new(name, J, dtype, tag)
+            nc.vector.tensor_copy(dst[:], table[:].indirect(offsets[:]))
+            return dst
+
+        xt_plane = zeroed_plane(nc.gpsimd, "xt_plane", T)
+        w_plane = zeroed_plane(nc.gpsimd, "w_plane", R)
+        xo_plane = zeroed_plane(nc.gpsimd, "xo_plane", Z)
+        w2_plane = zeroed_plane(nc.gpsimd, "w2_plane", R)
+        wb_plane = zeroed_plane(nc.gpsimd, "wb_plane", N)
+        ws_plane = zeroed_plane(nc.gpsimd, "ws_plane", N)
+        sx_plane = zeroed_plane(nc.gpsimd, "sx_plane", O)
+
+        l1 = load_list("l1", offs)
+        xt_w = load_words(nc.sync, "xt_w", xt_words[0], T, U16)
+        load_plane(nc.sync, xt_plane, xt_scales)
+        w_w = load_words(nc.sync, "w_w", fp8_words(w_words), R, U32)
+        load_plane(nc.sync, w_plane, w_scales)
+        l3 = load_list("l3", offs3)
+        l2 = load_list("l2", offs2)
+        xo_w = load_words(nc.sync, "xo_w", fp8_words(xo_words), Z, U32)
+        w2_w = load_words(nc.sync, "w2_w", fp8_words(w2_words), R, U32)
+        load_plane(nc.sync, xo_plane, xo_scales)
+        load_plane(nc.sync, w2_plane, w2_scales)
+        l4 = load_list("l4", offs4)
+        l5 = load_list("l5", offs5)
+
+        pw = [new("pw%d" % t, C, F32) for t in range(PACK)]
+        pv = [new("pv%d" % t, C, F32) for t in range(PACK)]
+
+        def first_stage(name, w_d, w_s, w_fmt, x_g, x_s, x_fmt):
+            banks = [ps.tile([P, J], F32, name=name + "0"), ps.tile([P, J], F32, name=name + "1")]
+            pair = ps.tile([P, 2, J], F32, name=name + "23")
+            sums = [banks[0][:], banks[1][:], pair[:, 0, :], pair[:, 1, :]]
+            for t in range(PACK):
+                cols = slice(t * P, (t + 1) * P)
+                nc.tensor.matmul_mx(
+                    sums[t], lhsT=w_d[:, cols].bitcast(w_fmt), lhsT_scale=w_s[:, cols],
+                    rhs=x_g[:].bitcast(x_fmt), rhs_scale=x_s[:], start=True, stop=True,
+                )
+            return sums
+
+        def place_vector(name, src, board, offsets):
+            vals = new(name, J, F32)
+            nc.vector.tensor_copy(vals[:], src)
+            nc.vector.tensor_copy(board[:].indirect(offsets[:]), vals[:])
+
+        def place_scalar(name, src, board, offsets, tag=""):
+            vals = new(name, J, F32, tag)
+            nc.scalar.activation(vals[:], src, ACT.Copy)
+            nc.scalar.activation(board[:].indirect(offsets[:]), vals[:], ACT.Copy)
+
+        hid = sb.tile([P, PACK, O], BF16, name="hid", align_bytes=64)
+
+        def add_boards(t):
+            pg = new("pg%d" % t, C, F32)
+            nc.vector.tensor_tensor(pg[:], pw[t][:], pv[t][:], ALU.add)
+            return pg
+
+        xt_g = gather("xt_g", xt_w, l1, U16)
+        w_d = deal(nc.vector.tensor_copy, "w_d", w_w, U32)
+        xt_gs = gather("xt_gs", xt_plane, l1, U8)
+        w_ds = deal(nc.vector.tensor_copy, "w_ds", w_plane, U8)
+        a = first_stage("a", w_d, w_ds, E5M2, xt_g, xt_gs, E2M1)
+        for t in range(PACK):
+            nc.vector.memset(pw[t][:].bitcast(I32), 0)
+        for t in range(PACK):
+            nc.vector.memset(pv[t][:].bitcast(I32), 0)
+        ws_w = load_words(nc.sync, "ws_w", fp8_words(ws_words), N, U32, "xt_w")
+        sx_w = load_words(nc.sync, "sx_w", fp8_words(sx_words), O, U32, "w_w")
+        wb_w = load_words(nc.sync, "wb_w", fp8_words(wb_words), N, U32, "xt_plane")
+        load_plane(nc.sync, ws_plane, ws_scales)
+        load_plane(nc.sync, sx_plane, sx_scales)
+        load_plane(nc.sync, wb_plane, wb_scales)
+        l6 = load_list("l6", offs6)
+        place_scalar("a0s", a[0], pw[0], l3)
+        place_vector("a1s", a[1], pw[1], l3)
+        w2_d = deal(nc.scalar.copy, "w2_d", w2_w, U32, "a0s")
+        xo_g = gather("xo_g", xo_w, l2, U32, "a1s")
+        xo_gs = gather("xo_gs", xo_plane, l2, U8, "xt_gs")
+        w2_ds = deal(nc.vector.tensor_copy, "w2_ds", w2_plane, U8, "w_ds")
+        b = first_stage("b", w2_d, w2_ds, E4M3, xo_g, xo_gs, E5M2)
+        place_scalar("a2s", a[2], pw[2], l3, "w2_w")
+        tz_t = []
+        for h, tag in enumerate(("xo_w", "w2_w")):
+            rows = new("tz%d" % h, E, F32, tag)
+            nc.sync.dma_start(rows[:], tz[h * P : (h + 1) * P, :])
+            tz_t.append(rows)
+        so_t = new("so_t", HALVES, F32, "w_plane")
+        bo_t = new("bo_t", HALVES, F32, "xo_plane")
+        with nc.allow_non_contiguous_dma(reason="one value a partition"):
+            nc.sync.dma_start(so_t[:], so.rearrange("(h p) o -> p (h o)", p=P))
+            nc.sync.dma_start(bo_t[:], bo.rearrange("(h p) o -> p (h o)", p=P))
+        acc = [ps.tile([P, O], F32, name="acc%d" % h) for h in range(HALVES)]
+        for h in range(HALVES):
+            cols = slice(h * P, (h + 1) * P)
+            nc.tensor.matmul_mx(
+                acc[h][:], lhsT=ws_w[:, cols].bitcast(E4M3), lhsT_scale=ws_plane[:, cols],
+                rhs=sx_w[:].bitcast(E5M2), rhs_scale=sx_plane[:], start=True, stop=False,
+            )
+        place_vector("b0s", b[0], pv[0], l4)
+        place_scalar("a3s", a[3], pw[3], l3)
+        pg0 = add_boards(0)
+        place_vector("b1s", b[1], pv[1], l4)
+        place_scalar("b2s", b[2], pv[2], l4)
+        place_scalar("b3s", b[3], pv[3], l4)
+        nc.scalar.activation(hid[:, 0, :], pg0[:].indirect(l5[:]), ACT.Copy)
+        for t in range(1, PACK):
+            pg = add_boards(t)
+            nc.vector.tensor_copy(hid[:, t, :], pg[:].indirect(l5[:]))
+
+        gate = []
+        for h in range(HALVES):
+            g = new("gate%d" % h, O, F32)
+            nc.scalar.activation(
+                g[:], tz_t[h][:].indirect(l6[:]), ACT.Sigmoid, bias=bo_t[:, h : h + 1], scale=so_t[:, h : h + 1]
+            )
+            gate.append(g)
+
+        woven = new("woven", PACK * O, BF16)
+        nc.vector.tensor_copy(
+            woven[:].rearrange("p (c i t) -> p c t i", i=4, t=PACK),
+            hid[:].rearrange("p t (c i) -> p c t i", i=4),
+        )
+        hq = new("hq", O, U32)
+        hq_s = new("hq_s", O, U8)
+        nc.vector.quantize_mx(hq[:].bitcast(E5M2), hq_s[:], woven[:])
+        for h in range(HALVES):
+            cols = slice(h * P, (h + 1) * P)
+            nc.tensor.matmul_mx(
+                acc[h][:], lhsT=wb_w[:, cols].bitcast(E4M3), lhsT_scale=wb_plane[:, cols],
+                rhs=hq[:].bitcast(E5M2), rhs_scale=hq_s[:], start=False, stop=True,
+            )
+        for h in range(HALVES):
+            y = new("y%d" % h, O, F32)
+            nc.vector.tensor_tensor(y[:], acc[h][:], gate[h][:], ALU.mult)
+            (nc.sync if h == 0 else nc.scalar).dma_start(out[h * P : (h + 1) * P, :], y[:])

@@ -62,6 +62,13 @@ def tile_list_twotab_shared_skip_finalgate_kernel(
             copy(dst[:].rearrange("p (t m) -> p m t", t=PACK), src[:].rearrange("p (m t) -> p m t", t=PACK))
             return dst
 
+        def deal_slow(name, src, dtype):
+            dst = new(name, R, dtype)
+            nc.gpsimd.tensor_copy(
+                dst[:].rearrange("p (t m) -> p t m", t=PACK), src[:].rearrange("p (m t) -> p t m", t=PACK)
+            )
+            return dst
+
         def gather(name, table, offsets, dtype, tag=""):
             dst = new(name, J, dtype, tag)
             nc.vector.tensor_copy(dst[:], table[:].indirect(offsets[:]))
@@ -71,9 +78,8 @@ def tile_list_twotab_shared_skip_finalgate_kernel(
         w_plane = zeroed_plane(nc.gpsimd, "w_plane", R)
         xo_plane = zeroed_plane(nc.gpsimd, "xo_plane", Z)
         w2_plane = zeroed_plane(nc.gpsimd, "w2_plane", R)
-        wb_plane = zeroed_plane(nc.gpsimd, "wb_plane", N)
-        ws_plane = zeroed_plane(nc.gpsimd, "ws_plane", N)
-        sx_plane = zeroed_plane(nc.gpsimd, "sx_plane", O)
+        late_planes = zeroed_plane(nc.gpsimd, "late_planes", 2 * N + O)
+        wb_plane, ws_plane, sx_plane = late_planes[:, :N], late_planes[:, N : 2 * N], late_planes[:, 2 * N :]
 
         l1 = load_list("l1", offs)
         xt_w = load_words(nc.sync, "xt_w", xt_words[0], T, U16)
@@ -90,45 +96,45 @@ def tile_list_twotab_shared_skip_finalgate_kernel(
         l5 = load_list("l5", offs5)
 
         pw = [new("pw%d" % t, C, F32) for t in range(PACK)]
-        pv = [new("pv%d" % t, C, F32) for t in range(PACK)]
+        pv = {t: new("pv%d" % t, C, F32) for t in (0, 2)}
 
-        def first_stage(name, w_d, w_s, w_fmt, x_g, x_s, x_fmt):
-            banks = [ps.tile([P, J], F32, name=name + "0"), ps.tile([P, J], F32, name=name + "1")]
-            pair = ps.tile([P, 2, J], F32, name=name + "23")
-            sums = [banks[0][:], banks[1][:], pair[:, 0, :], pair[:, 1, :]]
+        def first_stage(sums, w_d, w_s, w_fmt, x_g, x_s, x_fmt):
             for t in range(PACK):
                 cols = slice(t * P, (t + 1) * P)
                 nc.tensor.matmul_mx(
                     sums[t], lhsT=w_d[:, cols].bitcast(w_fmt), lhsT_scale=w_s[:, cols],
                     rhs=x_g[:].bitcast(x_fmt), rhs_scale=x_s[:], start=True, stop=True,
                 )
-            return sums
 
-        def place_vector(name, src, board, offsets):
-            vals = new(name, J, F32)
-            nc.vector.tensor_copy(vals[:], src)
-            nc.vector.tensor_copy(board[:].indirect(offsets[:]), vals[:])
+        def on_vector(dst, src):
+            nc.vector.tensor_copy(dst, src)
 
-        def place_scalar(name, src, board, offsets, tag=""):
-            vals = new(name, J, F32, tag)
-            nc.scalar.activation(vals[:], src, ACT.Copy)
-            nc.scalar.activation(board[:].indirect(offsets[:]), vals[:], ACT.Copy)
+        def on_scalar(dst, src):
+            nc.scalar.activation(dst, src, ACT.Copy)
+
+        def leave_psum(move, name, src, width, tag=""):
+            vals = new(name, width, F32, tag)
+            move(vals[:], src)
+            return vals
 
         hid = sb.tile([P, PACK, O], BF16, name="hid", align_bytes=64)
 
-        def add_boards(t):
+        def add_boards(engine, t):
             pg = new("pg%d" % t, C, F32)
-            nc.vector.tensor_tensor(pg[:], pw[t][:], pv[t][:], ALU.add)
+            engine.tensor_tensor(pg[:], pw[t][:], pv[t][:], ALU.add)
             return pg
 
         xt_g = gather("xt_g", xt_w, l1, U16)
         w_d = deal(nc.vector.tensor_copy, "w_d", w_w, U32)
         xt_gs = gather("xt_gs", xt_plane, l1, U8)
         w_ds = deal(nc.vector.tensor_copy, "w_ds", w_plane, U8)
-        a = first_stage("a", w_d, w_ds, E5M2, xt_g, xt_gs, E2M1)
+        a0 = ps.tile([P, J], F32, name="a0")
+        a1 = ps.tile([P, J], F32, name="a1")
+        a23 = ps.tile([P, 2 * J], F32, name="a23")
+        first_stage([a0[:], a1[:], a23[:, :J], a23[:, J:]], w_d, w_ds, E5M2, xt_g, xt_gs, E2M1)
         for t in range(PACK):
             nc.vector.memset(pw[t][:].bitcast(I32), 0)
-        for t in range(PACK):
+        for t in (0, 2):
             nc.vector.memset(pv[t][:].bitcast(I32), 0)
         ws_w = load_words(nc.sync, "ws_w", fp8_words(ws_words), N, U32, "xt_w")
         sx_w = load_words(nc.sync, "sx_w", fp8_words(sx_words), O, U32, "w_w")
@@ -137,24 +143,36 @@ def tile_list_twotab_shared_skip_finalgate_kernel(
         load_plane(nc.sync, sx_plane, sx_scales)
         load_plane(nc.sync, wb_plane, wb_scales)
         l6 = load_list("l6", offs6)
-        place_scalar("a0s", a[0], pw[0], l3)
-        place_vector("a1s", a[1], pw[1], l3)
-        w2_d = deal(nc.scalar.copy, "w2_d", w2_w, U32, "a0s")
+
+        a0s = leave_psum(on_scalar, "a0s", a0[:], J)
+        on_scalar(pw[0][:].indirect(l3[:]), a0s[:])
+        a1s = leave_psum(on_vector, "a1s", a1[:], J)
+        on_vector(pw[1][:].indirect(l3[:]), a1s[:])
+        w2_d = deal_slow("w2_d", w2_w, U32)
         xo_g = gather("xo_g", xo_w, l2, U32, "a1s")
         xo_gs = gather("xo_gs", xo_plane, l2, U8, "xt_gs")
-        w2_ds = deal(nc.vector.tensor_copy, "w2_ds", w2_plane, U8, "w_ds")
-        b = first_stage("b", w2_d, w2_ds, E4M3, xo_g, xo_gs, E5M2)
-        place_scalar("a2s", a[2], pw[2], l3, "w2_w")
+        w2_ds = deal_slow("w2_ds", w2_plane, U8)
+        for t, tag in ((1, "w2_w"), (3, "w2_plane")):
+            pv[t] = new("pv%d" % t, C, F32, tag)
+            nc.gpsimd.memset(pv[t][:].bitcast(I32), 0)
+        b01 = ps.tile([P, 2 * J], F32, name="b01")
+        b23 = ps.tile([P, 2 * J], F32, name="b23")
+        first_stage([b01[:, :J], b01[:, J:], b23[:, :J], b23[:, J:]], w2_d, w2_ds, E4M3, xo_g, xo_gs, E5M2)
+        a2s = leave_psum(on_scalar, "a2s", a23[:, :J], J)
+        on_scalar(pw[2][:].indirect(l3[:]), a2s[:])
+        a3s = leave_psum(on_vector, "a3s", a23[:, J:], J, "xo_plane")
+        on_vector(pw[3][:].indirect(l3[:]), a3s[:])
         tz_t = []
-        for h, tag in enumerate(("xo_w", "w2_w")):
+        for h, tag in enumerate(("xo_w", "w_d")):
             rows = new("tz%d" % h, E, F32, tag)
             nc.sync.dma_start(rows[:], tz[h * P : (h + 1) * P, :])
             tz_t.append(rows)
         so_t = new("so_t", HALVES, F32, "w_plane")
-        bo_t = new("bo_t", HALVES, F32, "xo_plane")
+        bo_t = new("bo_t", HALVES, F32, "w_ds")
         with nc.allow_non_contiguous_dma(reason="one value a partition"):
             nc.sync.dma_start(so_t[:], so.rearrange("(h p) o -> p (h o)", p=P))
             nc.sync.dma_start(bo_t[:], bo.rearrange("(h p) o -> p (h o)", p=P))
+
         acc = [ps.tile([P, O], F32, name="acc%d" % h) for h in range(HALVES)]
         for h in range(HALVES):
             cols = slice(h * P, (h + 1) * P)
@@ -162,16 +180,18 @@ def tile_list_twotab_shared_skip_finalgate_kernel(
                 acc[h][:], lhsT=ws_w[:, cols].bitcast(E4M3), lhsT_scale=ws_plane[:, cols],
                 rhs=sx_w[:].bitcast(E5M2), rhs_scale=sx_plane[:], start=True, stop=False,
             )
-        place_vector("b0s", b[0], pv[0], l4)
-        place_scalar("a3s", a[3], pw[3], l3)
-        pg0 = add_boards(0)
-        place_vector("b1s", b[1], pv[1], l4)
-        place_scalar("b2s", b[2], pv[2], l4)
-        place_scalar("b3s", b[3], pv[3], l4)
-        nc.scalar.activation(hid[:, 0, :], pg0[:].indirect(l5[:]), ACT.Copy)
-        for t in range(1, PACK):
-            pg = add_boards(t)
-            nc.vector.tensor_copy(hid[:, t, :], pg[:].indirect(l5[:]))
+        b01s = leave_psum(on_scalar, "b01s", b01[:], 2 * J)
+        b23s = leave_psum(on_vector, "b23s", b23[:], 2 * J)
+        on_scalar(pv[0][:].indirect(l4[:]), b01s[:, :J])
+        on_vector(pv[2][:].indirect(l4[:]), b23s[:, :J])
+        on_scalar(pv[1][:].indirect(l4[:]), b01s[:, J:])
+        on_vector(pv[3][:].indirect(l4[:]), b23s[:, J:])
+        pg = {t: add_boards(nc.gpsimd, t) for t in (0, 2)}
+        pg[1] = add_boards(nc.vector, 1)
+        pg[3] = add_boards(nc.vector, 3)
+        for t in (0, 2, 1):
+            on_scalar(hid[:, t, :], pg[t][:].indirect(l5[:]))
+        on_vector(hid[:, 3, :], pg[3][:].indirect(l5[:]))
 
         gate = []
         for h in range(HALVES):

@@ -98,8 +98,8 @@ def tile_list_twotab_shared_skip_finalgate_kernel(
         pw = [new("pw%d" % t, C, F32) for t in range(PACK)]
         pv = {t: new("pv%d" % t, C, F32) for t in (0, 2)}
 
-        def first_stage(sums, w_d, w_s, w_fmt, x_g, x_s, x_fmt):
-            for t in range(PACK):
+        def first_stage(sums, order, w_d, w_s, w_fmt, x_g, x_s, x_fmt):
+            for t in order:
                 cols = slice(t * P, (t + 1) * P)
                 nc.tensor.matmul_mx(
                     sums[t], lhsT=w_d[:, cols].bitcast(w_fmt), lhsT_scale=w_s[:, cols],
@@ -128,10 +128,8 @@ def tile_list_twotab_shared_skip_finalgate_kernel(
         w_d = deal(nc.vector.tensor_copy, "w_d", w_w, U32)
         xt_gs = gather("xt_gs", xt_plane, l1, U8)
         w_ds = deal(nc.vector.tensor_copy, "w_ds", w_plane, U8)
-        a0 = ps.tile([P, J], F32, name="a0")
-        a1 = ps.tile([P, J], F32, name="a1")
-        a23 = ps.tile([P, 2 * J], F32, name="a23")
-        first_stage([a0[:], a1[:], a23[:, :J], a23[:, J:]], w_d, w_ds, E5M2, xt_g, xt_gs, E2M1)
+        a = [ps.tile([P, J], F32, name="a%d" % t) for t in range(PACK)]
+        first_stage([bank[:] for bank in a], (1, 0, 2, 3), w_d, w_ds, E5M2, xt_g, xt_gs, E2M1)
         for t in range(PACK):
             nc.vector.memset(pw[t][:].bitcast(I32), 0)
         for t in (0, 2):
@@ -144,9 +142,10 @@ def tile_list_twotab_shared_skip_finalgate_kernel(
         load_plane(nc.sync, wb_plane, wb_scales)
         l6 = load_list("l6", offs6)
 
-        a0s = leave_psum(on_scalar, "a0s", a0[:], J)
+        a0s = leave_psum(on_scalar, "a0s", a[0][:], J)
+        a2s = leave_psum(on_scalar, "a2s", a[2][:], J)
         on_scalar(pw[0][:].indirect(l3[:]), a0s[:])
-        a1s = leave_psum(on_vector, "a1s", a1[:], J)
+        a1s = leave_psum(on_vector, "a1s", a[1][:], J)
         on_vector(pw[1][:].indirect(l3[:]), a1s[:])
         w2_d = deal_slow("w2_d", w2_w, U32)
         xo_g = gather("xo_g", xo_w, l2, U32, "a1s")
@@ -155,12 +154,11 @@ def tile_list_twotab_shared_skip_finalgate_kernel(
         for t, tag in ((1, "w2_w"), (3, "w2_plane")):
             pv[t] = new("pv%d" % t, C, F32, tag)
             nc.gpsimd.memset(pv[t][:].bitcast(I32), 0)
-        b01 = ps.tile([P, 2 * J], F32, name="b01")
-        b23 = ps.tile([P, 2 * J], F32, name="b23")
-        first_stage([b01[:, :J], b01[:, J:], b23[:, :J], b23[:, J:]], w2_d, w2_ds, E4M3, xo_g, xo_gs, E5M2)
-        a2s = leave_psum(on_scalar, "a2s", a23[:, :J], J)
+        b01 = ps.tile([P, 2 * J], F32, name="b01", tag="b01")
+        b23 = ps.tile([P, 2 * J], F32, name="b23", tag="b23")
+        first_stage([b01[:, :J], b01[:, J:], b23[:, :J], b23[:, J:]], range(PACK), w2_d, w2_ds, E4M3, xo_g, xo_gs, E5M2)
         on_scalar(pw[2][:].indirect(l3[:]), a2s[:])
-        a3s = leave_psum(on_vector, "a3s", a23[:, J:], J, "xo_plane")
+        a3s = leave_psum(on_vector, "a3s", a[3][:], J, "xo_plane")
         on_vector(pw[3][:].indirect(l3[:]), a3s[:])
         tz_t = []
         for h, tag in enumerate(("xo_w", "w_d")):
@@ -173,25 +171,29 @@ def tile_list_twotab_shared_skip_finalgate_kernel(
             nc.sync.dma_start(so_t[:], so.rearrange("(h p) o -> p (h o)", p=P))
             nc.sync.dma_start(bo_t[:], bo.rearrange("(h p) o -> p (h o)", p=P))
 
-        acc = [ps.tile([P, O], F32, name="acc%d" % h) for h in range(HALVES)]
+        b01s = leave_psum(on_scalar, "b01s", b01[:], 2 * J)
+        b23s = leave_psum(on_scalar, "b23s", b23[:], 2 * J)
+        acc = [ps.tile([P, O], F32, name="acc%d" % h, tag=tag) for h, tag in enumerate(("b01", "b23"))]
         for h in range(HALVES):
             cols = slice(h * P, (h + 1) * P)
             nc.tensor.matmul_mx(
                 acc[h][:], lhsT=ws_w[:, cols].bitcast(E4M3), lhsT_scale=ws_plane[:, cols],
                 rhs=sx_w[:].bitcast(E5M2), rhs_scale=sx_plane[:], start=True, stop=False,
             )
-        b01s = leave_psum(on_scalar, "b01s", b01[:], 2 * J)
-        b23s = leave_psum(on_vector, "b23s", b23[:], 2 * J)
         on_scalar(pv[0][:].indirect(l4[:]), b01s[:, :J])
         on_vector(pv[2][:].indirect(l4[:]), b23s[:, :J])
         on_scalar(pv[1][:].indirect(l4[:]), b01s[:, J:])
         on_vector(pv[3][:].indirect(l4[:]), b23s[:, J:])
-        pg = {t: add_boards(nc.gpsimd, t) for t in (0, 2)}
-        pg[1] = add_boards(nc.vector, 1)
-        pg[3] = add_boards(nc.vector, 3)
-        for t in (0, 2, 1):
+        pg = {0: add_boards(nc.gpsimd, 0)}
+        for t in (2, 1, 3):
+            pg[t] = add_boards(nc.vector, t)
+        parts = [slice(i * P, (i + 1) * P) for i in range(O // P)]
+        for t in (0, 2):
             on_scalar(hid[:, t, :], pg[t][:].indirect(l5[:]))
-        on_vector(hid[:, 3, :], pg[3][:].indirect(l5[:]))
+        for cols in parts:
+            entries = l5[:, cols.start // 16 : cols.stop // 16]
+            on_scalar(hid[:, 1, cols], pg[1][:].indirect(entries))
+            on_vector(hid[:, 3, cols], pg[3][:].indirect(entries))
 
         gate = []
         for h in range(HALVES):
@@ -201,20 +203,22 @@ def tile_list_twotab_shared_skip_finalgate_kernel(
             )
             gate.append(g)
 
-        woven = new("woven", PACK * O, BF16)
-        nc.vector.tensor_copy(
-            woven[:].rearrange("p (c i t) -> p c t i", i=4, t=PACK),
-            hid[:].rearrange("p t (c i) -> p c t i", i=4),
-        )
-        hq = new("hq", O, U32)
-        hq_s = new("hq_s", O, U8)
-        nc.vector.quantize_mx(hq[:].bitcast(E5M2), hq_s[:], woven[:])
-        for h in range(HALVES):
-            cols = slice(h * P, (h + 1) * P)
-            nc.tensor.matmul_mx(
-                acc[h][:], lhsT=wb_w[:, cols].bitcast(E4M3), lhsT_scale=wb_plane[:, cols],
-                rhs=hq[:].bitcast(E5M2), rhs_scale=hq_s[:], start=False, stop=True,
+        woven = [new("woven%d" % i, PACK * P, BF16) for i in range(O // P)]
+        for i, cols in enumerate(parts):
+            nc.vector.tensor_copy(
+                woven[i][:].rearrange("p (c i t) -> p c t i", i=4, t=PACK),
+                hid[:, :, cols].rearrange("p t (c i) -> p c t i", i=4),
             )
+        for i, cols in enumerate(parts):
+            hq = new("hq%d" % i, P, U32)
+            hq_s = new("hq_s%d" % i, P, U8)
+            nc.vector.quantize_mx(hq[:].bitcast(E5M2), hq_s[:], woven[i][:])
+            for h in range(HALVES):
+                rows = slice(h * P, (h + 1) * P)
+                nc.tensor.matmul_mx(
+                    acc[h][:, cols], lhsT=wb_w[:, rows].bitcast(E4M3), lhsT_scale=wb_plane[:, rows],
+                    rhs=hq[:].bitcast(E5M2), rhs_scale=hq_s[:], start=False, stop=(i == O // P - 1),
+                )
         for h in range(HALVES):
             y = new("y%d" % h, O, F32)
             nc.vector.tensor_tensor(y[:], acc[h][:], gate[h][:], ALU.mult)

@@ -81,6 +81,11 @@ def tile_list_twotab_shared_skip_finalgate_kernel(
         late_planes = zeroed_plane(nc.gpsimd, "late_planes", 2 * N + O)
         wb_plane, ws_plane, sx_plane = late_planes[:, :N], late_planes[:, N : 2 * N], late_planes[:, 2 * N :]
 
+        warm_in = new("warm_in", 1, F32)
+        warm_out = new("warm_out", 1, F32)
+        nc.vector.memset(warm_in[:], 0.0)
+        nc.scalar.activation(warm_out[:], warm_in[:], ACT.Sigmoid)
+
         l1 = load_list("l1", offs)
         xt_w = load_words(nc.sync, "xt_w", xt_words[0], T, U16)
         load_plane(nc.sync, xt_plane, xt_scales)

@@ -19,7 +19,11 @@ ALU = mybir.AluOpType
 
 P = 128
 PACK = 4
-HALVES = N // P
+QUADRANT = 32
+PER_COLUMN = 16
+ROW_TILES = N // P
+PARTS = O // P
+RUN = 4
 
 
 def tile_list_twotab_shared_skip_finalgate_kernel(
@@ -36,79 +40,49 @@ def tile_list_twotab_shared_skip_finalgate_kernel(
             return sb.tile([P, width], dtype, name=name, tag=tag or name, align_bytes=64)
 
         def load_list(name, src):
-            dst = sb.tile([P, J // 16], U16, name=name)
+            dst = sb.tile([P, J // PER_COLUMN], U16, name=name)
             nc.sync.dma_start(dst[:], src)
             return dst
 
-        def load_words(queue, name, src, width, dtype, tag=""):
+        def load_words(name, src, width, dtype, tag=""):
             dst = new(name, width, dtype, tag)
-            queue.dma_start(dst[:].bitcast(I32), src.bitcast(I32))
+            nc.sync.dma_start(dst[:].bitcast(I32), src.bitcast(I32))
             return dst
-
-        def zeroed_plane(engine, name, width):
-            plane = new(name, width, U8)
-            engine.memset(plane[:].bitcast(I32), 0)
-            return plane
-
-        def load_plane(queue, plane, src):
-            for q in range(4):
-                queue.dma_start(plane[32 * q : 32 * q + 4, :].bitcast(I32), src[0, 4 * q : 4 * q + 4, :].bitcast(I32))
 
         def fp8_words(src):
             return src[0].rearrange("p c r -> p (c r)")
 
-        def deal(copy, name, src, dtype, tag=""):
-            dst = new(name, R, dtype, tag)
-            copy(dst[:].rearrange("p (t m) -> p m t", t=PACK), src[:].rearrange("p (m t) -> p m t", t=PACK))
-            return dst
+        def zeroed_plane(name, width):
+            plane = new(name, width, U8)
+            nc.gpsimd.memset(plane[:].bitcast(I32), 0)
+            return plane
 
-        def deal_slow(name, src, dtype):
+        def load_plane(plane, src):
+            for q in range(P // QUADRANT):
+                nc.sync.dma_start(
+                    plane[QUADRANT * q : QUADRANT * q + 4, :].bitcast(I32),
+                    src[0, 4 * q : 4 * q + 4, :].bitcast(I32),
+                )
+
+        def deal(copy, walk, name, src, dtype):
             dst = new(name, R, dtype)
-            nc.gpsimd.tensor_copy(
-                dst[:].rearrange("p (t m) -> p t m", t=PACK), src[:].rearrange("p (m t) -> p t m", t=PACK)
+            copy(
+                dst[:].rearrange("p (t m) -> p " + walk, t=PACK),
+                src[:].rearrange("p (m t) -> p " + walk, t=PACK),
             )
             return dst
 
-        def gather(name, table, offsets, dtype, tag=""):
+        def gather_packed(name, table, entries, dtype, tag=""):
             dst = new(name, J, dtype, tag)
-            nc.vector.tensor_copy(dst[:], table[:].indirect(offsets[:]))
+            nc.vector.tensor_copy(dst[:], table[:].indirect(entries[:]))
             return dst
 
-        xt_plane = zeroed_plane(nc.gpsimd, "xt_plane", T)
-        w_plane = zeroed_plane(nc.gpsimd, "w_plane", R)
-        xo_plane = zeroed_plane(nc.gpsimd, "xo_plane", Z)
-        w2_plane = zeroed_plane(nc.gpsimd, "w2_plane", R)
-        late_planes = zeroed_plane(nc.gpsimd, "late_planes", 2 * N + O)
-        wb_plane, ws_plane, sx_plane = late_planes[:, :N], late_planes[:, N : 2 * N], late_planes[:, 2 * N :]
-
-        warm_in = new("warm_in", 1, F32)
-        warm_out = new("warm_out", 1, F32)
-        nc.vector.memset(warm_in[:], 0.0)
-        nc.scalar.activation(warm_out[:], warm_in[:], ACT.Sigmoid)
-
-        l1 = load_list("l1", offs)
-        xt_w = load_words(nc.sync, "xt_w", xt_words[0], T, U16)
-        load_plane(nc.sync, xt_plane, xt_scales)
-        w_w = load_words(nc.sync, "w_w", fp8_words(w_words), R, U32)
-        load_plane(nc.sync, w_plane, w_scales)
-        l3 = load_list("l3", offs3)
-        l2 = load_list("l2", offs2)
-        xo_w = load_words(nc.sync, "xo_w", fp8_words(xo_words), Z, U32)
-        w2_w = load_words(nc.sync, "w2_w", fp8_words(w2_words), R, U32)
-        load_plane(nc.sync, xo_plane, xo_scales)
-        load_plane(nc.sync, w2_plane, w2_scales)
-        l4 = load_list("l4", offs4)
-        l5 = load_list("l5", offs5)
-
-        pw = [new("pw%d" % t, C, F32) for t in range(PACK)]
-        pv = {t: new("pv%d" % t, C, F32) for t in (0, 2)}
-
-        def first_stage(sums, order, w_d, w_s, w_fmt, x_g, x_s, x_fmt):
+        def first_stage(sums, order, weights, weight_scales, weight_fmt, picked, picked_scales, picked_fmt):
             for t in order:
                 cols = slice(t * P, (t + 1) * P)
                 nc.tensor.matmul_mx(
-                    sums[t], lhsT=w_d[:, cols].bitcast(w_fmt), lhsT_scale=w_s[:, cols],
-                    rhs=x_g[:].bitcast(x_fmt), rhs_scale=x_s[:], start=True, stop=True,
+                    sums[t], lhsT=weights[:, cols].bitcast(weight_fmt), lhsT_scale=weight_scales[:, cols],
+                    rhs=picked[:].bitcast(picked_fmt), rhs_scale=picked_scales[:], start=True, stop=True,
                 )
 
         def on_vector(dst, src):
@@ -122,109 +96,148 @@ def tile_list_twotab_shared_skip_finalgate_kernel(
             move(vals[:], src)
             return vals
 
+        xt_plane = zeroed_plane("xt_plane", T)
+        w_plane = zeroed_plane("w_plane", R)
+        xo_plane = zeroed_plane("xo_plane", Z)
+        w2_plane = zeroed_plane("w2_plane", R)
+        second_planes = zeroed_plane("second_planes", 2 * N + O)
+        wb_plane, ws_plane, sx_plane = second_planes[:, :N], second_planes[:, N : 2 * N], second_planes[:, 2 * N :]
+
+        warm_in = new("warm_in", 1, F32)
+        warm_out = new("warm_out", 1, F32)
+        nc.vector.memset(warm_in[:], 0.0)
+        nc.scalar.activation(warm_out[:], warm_in[:], ACT.Sigmoid)
+
+        idx = load_list("idx", offs)
+        xt_w = load_words("xt_w", xt_words[0], T, U16)
+        load_plane(xt_plane, xt_scales)
+        w_w = load_words("w_w", fp8_words(w_words), R, U32)
+        load_plane(w_plane, w_scales)
+        idx3 = load_list("idx3", offs3)
+        idx2 = load_list("idx2", offs2)
+        xo_w = load_words("xo_w", fp8_words(xo_words), Z, U32)
+        w2_w = load_words("w2_w", fp8_words(w2_words), R, U32)
+        load_plane(xo_plane, xo_scales)
+        load_plane(w2_plane, w2_scales)
+        idx4 = load_list("idx4", offs4)
+        idx5 = load_list("idx5", offs5)
+
+        pw = [new("pw%d" % t, C, F32) for t in range(PACK)]
+        pv = {t: new("pv%d" % t, C, F32) for t in (0, 2)}
         hid = sb.tile([P, PACK, O], BF16, name="hid", align_bytes=64)
 
         def add_boards(engine, t):
-            pg = new("pg%d" % t, C, F32)
-            engine.tensor_tensor(pg[:], pw[t][:], pv[t][:], ALU.add)
-            return pg
+            whole = new("pg%d" % t, C, F32)
+            engine.tensor_tensor(whole[:], pw[t][:], pv[t][:], ALU.add)
+            return whole
 
-        xt_g = gather("xt_g", xt_w, l1, U16)
-        w_d = deal(nc.vector.tensor_copy, "w_d", w_w, U32)
-        xt_gs = gather("xt_gs", xt_plane, l1, U8)
-        w_ds = deal(nc.vector.tensor_copy, "w_ds", w_plane, U8)
+        xt_g = gather_packed("xt_g", xt_w, idx, U16)
+        w_dealt = deal(nc.scalar.copy, "m t", "w_dealt", w_w, U32)
+        xt_gs = gather_packed("xt_gs", xt_plane, idx, U8)
+        w_dealt_s = deal(nc.vector.tensor_copy, "m t", "w_dealt_s", w_plane, U8)
         a = [ps.tile([P, J], F32, name="a%d" % t) for t in range(PACK)]
-        first_stage([bank[:] for bank in a], (1, 0, 2, 3), w_d, w_ds, E5M2, xt_g, xt_gs, E2M1)
+        first_stage([bank[:] for bank in a], (1, 0, 2, 3), w_dealt, w_dealt_s, E5M2, xt_g, xt_gs, E2M1)
+
         for t in range(PACK):
             nc.vector.memset(pw[t][:].bitcast(I32), 0)
         for t in (0, 2):
             nc.vector.memset(pv[t][:].bitcast(I32), 0)
-        ws_w = load_words(nc.sync, "ws_w", fp8_words(ws_words), N, U32, "xt_w")
-        sx_w = load_words(nc.sync, "sx_w", fp8_words(sx_words), O, U32, "w_w")
-        wb_w = load_words(nc.sync, "wb_w", fp8_words(wb_words), N, U32, "xt_plane")
-        load_plane(nc.sync, ws_plane, ws_scales)
-        load_plane(nc.sync, sx_plane, sx_scales)
-        load_plane(nc.sync, wb_plane, wb_scales)
-        l6 = load_list("l6", offs6)
+
+        ws_w = load_words("ws_w", fp8_words(ws_words), N, U32, "xt_w")
+        sx_w = load_words("sx_w", fp8_words(sx_words), O, U32, "w_w")
+        wb_w = load_words("wb_w", fp8_words(wb_words), N, U32, "xt_plane")
+        load_plane(ws_plane, ws_scales)
+        load_plane(sx_plane, sx_scales)
+        load_plane(wb_plane, wb_scales)
+        idx6 = load_list("idx6", offs6)
 
         a0s = leave_psum(on_scalar, "a0s", a[0][:], J)
         a2s = leave_psum(on_scalar, "a2s", a[2][:], J)
-        on_scalar(pw[0][:].indirect(l3[:]), a0s[:])
+        on_scalar(pw[0][:].indirect(idx3[:]), a0s[:])
         a1s = leave_psum(on_vector, "a1s", a[1][:], J)
-        on_vector(pw[1][:].indirect(l3[:]), a1s[:])
-        w2_d = deal_slow("w2_d", w2_w, U32)
-        xo_g = gather("xo_g", xo_w, l2, U32, "a1s")
-        xo_gs = gather("xo_gs", xo_plane, l2, U8, "xt_gs")
-        w2_ds = deal_slow("w2_ds", w2_plane, U8)
+        on_vector(pw[1][:].indirect(idx3[:]), a1s[:])
+        w2_dealt = deal(nc.gpsimd.tensor_copy, "t m", "w2_dealt", w2_w, U32)
+        xo_g = gather_packed("xo_g", xo_w, idx2, U32, "a1s")
+        xo_gs = gather_packed("xo_gs", xo_plane, idx2, U8, "xt_gs")
+        w2_dealt_s = deal(nc.gpsimd.tensor_copy, "t m", "w2_dealt_s", w2_plane, U8)
         for t, tag in ((1, "w2_w"), (3, "w2_plane")):
             pv[t] = new("pv%d" % t, C, F32, tag)
             nc.gpsimd.memset(pv[t][:].bitcast(I32), 0)
         b01 = ps.tile([P, 2 * J], F32, name="b01", tag="b01")
         b23 = ps.tile([P, 2 * J], F32, name="b23", tag="b23")
-        first_stage([b01[:, :J], b01[:, J:], b23[:, :J], b23[:, J:]], range(PACK), w2_d, w2_ds, E4M3, xo_g, xo_gs, E5M2)
-        on_scalar(pw[2][:].indirect(l3[:]), a2s[:])
+        b = [b01[:, :J], b01[:, J:], b23[:, :J], b23[:, J:]]
+        first_stage(b, range(PACK), w2_dealt, w2_dealt_s, E4M3, xo_g, xo_gs, E5M2)
+        on_scalar(pw[2][:].indirect(idx3[:]), a2s[:])
         a3s = leave_psum(on_vector, "a3s", a[3][:], J, "xo_plane")
-        on_vector(pw[3][:].indirect(l3[:]), a3s[:])
-        tz_t = []
-        for h, tag in enumerate(("xo_w", "w_d")):
-            rows = new("tz%d" % h, E, F32, tag)
-            nc.sync.dma_start(rows[:], tz[h * P : (h + 1) * P, :])
-            tz_t.append(rows)
-        so_t = new("so_t", HALVES, F32, "w_plane")
-        bo_t = new("bo_t", HALVES, F32, "w_ds")
-        with nc.allow_non_contiguous_dma(reason="one value a partition"):
-            nc.sync.dma_start(so_t[:], so.rearrange("(h p) o -> p (h o)", p=P))
-            nc.sync.dma_start(bo_t[:], bo.rearrange("(h p) o -> p (h o)", p=P))
+        on_vector(pw[3][:].indirect(idx3[:]), a3s[:])
+
+        tz_rows = []
+        for h, tag in enumerate(("xo_w", "w_dealt")):
+            table = new("tz%d" % h, E, F32, tag)
+            nc.sync.dma_start(table[:], tz[h * P : (h + 1) * P, :])
+            tz_rows.append(table)
+        slope = new("slope", ROW_TILES, F32, "w_plane")
+        offset = new("offset", ROW_TILES, F32, "w_dealt_s")
+        with nc.allow_non_contiguous_dma(reason="one value a partition for each tile of output features"):
+            nc.sync.dma_start(slope[:], so.rearrange("(h p) o -> p (h o)", p=P))
+            nc.sync.dma_start(offset[:], bo.rearrange("(h p) o -> p (h o)", p=P))
 
         b01s = leave_psum(on_scalar, "b01s", b01[:], 2 * J)
         b23s = leave_psum(on_scalar, "b23s", b23[:], 2 * J)
-        acc = [ps.tile([P, O], F32, name="acc%d" % h, tag=tag) for h, tag in enumerate(("b01", "b23"))]
-        for h in range(HALVES):
-            cols = slice(h * P, (h + 1) * P)
-            nc.tensor.matmul_mx(
-                acc[h][:], lhsT=ws_w[:, cols].bitcast(E4M3), lhsT_scale=ws_plane[:, cols],
-                rhs=sx_w[:].bitcast(E5M2), rhs_scale=sx_plane[:], start=True, stop=False,
-            )
-        on_scalar(pv[0][:].indirect(l4[:]), b01s[:, :J])
-        on_vector(pv[2][:].indirect(l4[:]), b23s[:, :J])
-        on_scalar(pv[1][:].indirect(l4[:]), b01s[:, J:])
-        on_vector(pv[3][:].indirect(l4[:]), b23s[:, J:])
+
+        parts = [slice(i * P, (i + 1) * P) for i in range(PARTS)]
+        acc = [ps.tile([P, ROW_TILES, P], F32, name="acc%d" % i, tag=tag) for i, tag in enumerate(("b01", "b23"))]
+        for i, cols in enumerate(parts):
+            for h in range(ROW_TILES):
+                rows = slice(h * P, (h + 1) * P)
+                nc.tensor.matmul_mx(
+                    acc[i][:, h, :], lhsT=ws_w[:, rows].bitcast(E4M3), lhsT_scale=ws_plane[:, rows],
+                    rhs=sx_w[:, cols].bitcast(E5M2), rhs_scale=sx_plane[:, cols], start=(h == 0), stop=False,
+                )
+
+        half = J // 2
+        on_scalar(pv[0][:].indirect(idx4[:]), b01s[:, :J])
+        on_vector(pv[2][:].indirect(idx4[:]), b23s[:, :J])
+        on_scalar(pv[1][:].indirect(idx4[:]), b01s[:, J:])
+        on_vector(pv[3][:].indirect(idx4[:, : half // PER_COLUMN]), b23s[:, J : J + half])
+        on_scalar(pv[3][:].indirect(idx4[:, half // PER_COLUMN :]), b23s[:, J + half :])
         pg = {0: add_boards(nc.gpsimd, 0)}
         for t in (2, 1, 3):
             pg[t] = add_boards(nc.vector, t)
-        parts = [slice(i * P, (i + 1) * P) for i in range(O // P)]
+
         for t in (0, 2):
-            on_scalar(hid[:, t, :], pg[t][:].indirect(l5[:]))
+            on_scalar(hid[:, t, :], pg[t][:].indirect(idx5[:]))
         for cols in parts:
-            entries = l5[:, cols.start // 16 : cols.stop // 16]
+            entries = idx5[:, cols.start // PER_COLUMN : cols.stop // PER_COLUMN]
             on_scalar(hid[:, 1, cols], pg[1][:].indirect(entries))
             on_vector(hid[:, 3, cols], pg[3][:].indirect(entries))
 
-        gate = []
-        for h in range(HALVES):
-            g = new("gate%d" % h, O, F32)
+        gate = sb.tile([P, ROW_TILES, O], F32, name="gate", align_bytes=64)
+        for h in range(ROW_TILES):
             nc.scalar.activation(
-                g[:], tz_t[h][:].indirect(l6[:]), ACT.Sigmoid, bias=bo_t[:, h : h + 1], scale=so_t[:, h : h + 1]
+                gate[:, h, :], tz_rows[h][:].indirect(idx6[:]), ACT.Sigmoid,
+                bias=offset[:, h : h + 1], scale=slope[:, h : h + 1],
             )
-            gate.append(g)
 
-        woven = [new("woven%d" % i, PACK * P, BF16) for i in range(O // P)]
+        woven = [new("woven%d" % i, PACK * P, BF16) for i in range(PARTS)]
         for i, cols in enumerate(parts):
             nc.vector.tensor_copy(
-                woven[i][:].rearrange("p (c i t) -> p c t i", i=4, t=PACK),
-                hid[:, :, cols].rearrange("p t (c i) -> p c t i", i=4),
+                woven[i][:].rearrange("p (c n t) -> p c t n", n=RUN, t=PACK),
+                hid[:, :, cols].rearrange("p t (c n) -> p c t n", n=RUN),
             )
-        for i, cols in enumerate(parts):
-            hq = new("hq%d" % i, P, U32)
-            hq_s = new("hq_s%d" % i, P, U8)
-            nc.vector.quantize_mx(hq[:].bitcast(E5M2), hq_s[:], woven[i][:])
-            for h in range(HALVES):
+        for i in range(PARTS):
+            hid_codes = new("hid_codes%d" % i, P, U32)
+            hid_plane = new("hid_plane%d" % i, P, U8)
+            nc.vector.quantize_mx(hid_codes[:].bitcast(E5M2), hid_plane[:], woven[i][:])
+            for h in range(ROW_TILES):
                 rows = slice(h * P, (h + 1) * P)
                 nc.tensor.matmul_mx(
-                    acc[h][:, cols], lhsT=wb_w[:, rows].bitcast(E4M3), lhsT_scale=wb_plane[:, rows],
-                    rhs=hq[:].bitcast(E5M2), rhs_scale=hq_s[:], start=False, stop=(i == O // P - 1),
+                    acc[i][:, h, :], lhsT=wb_w[:, rows].bitcast(E4M3), lhsT_scale=wb_plane[:, rows],
+                    rhs=hid_codes[:].bitcast(E5M2), rhs_scale=hid_plane[:], start=False, stop=(h == ROW_TILES - 1),
                 )
-        for h in range(HALVES):
-            y = new("y%d" % h, O, F32)
-            nc.vector.tensor_tensor(y[:], acc[h][:], gate[h][:], ALU.mult)
-            (nc.sync if h == 0 else nc.scalar).dma_start(out[h * P : (h + 1) * P, :], y[:])
+
+        out_rows = out.rearrange("(h p) o -> p h o", p=P)
+        for i, cols in enumerate(parts):
+            y = sb.tile([P, ROW_TILES, P], F32, name="y%d" % i, align_bytes=64)
+            nc.vector.tensor_tensor(y[:], acc[i][:], gate[:, :, cols], ALU.mult)
+            nc.sync.dma_start(out_rows[:, :, cols], y[:])

from contextlib import ExitStack

import concourse.mybir as mybir

K, F, T, Z, J, R, C, O, N, L, E = 512, 512, 1024, 1024, 256, 512, 512, 256, 256, 512, 1024
FLOPS = 2 * (K * R * J + F * R * J + R * N * O + L * N * O)

F32 = mybir.dt.float32
BF16 = mybir.dt.bfloat16
I32 = mybir.dt.int32
U32 = mybir.dt.uint32
U16 = mybir.dt.uint16
U8 = mybir.dt.uint8
E4M3 = mybir.dt.float8_e4m3fn_x4
E5M2 = mybir.dt.float8_e5m2_x4
E2M1 = mybir.dt.float4_e2m1fn_x4
ACT = mybir.ActivationFunctionType
ALU = mybir.AluOpType

P = 128
PACK = 4
QUADRANT = 32
PER_COLUMN = 16
ROW_TILES = N // P
PARTS = O // P
RUN = 4


def tile_list_twotab_shared_skip_finalgate_kernel(
    tc, xt_words, xt_scales, w_words, w_scales, xo_words, xo_scales, w2_words, w2_scales,
    wb_words, wb_scales, sx_words, sx_scales, ws_words, ws_scales, tz, so, bo,
    offs, offs2, offs3, offs4, offs5, offs6, out,
):
    nc = tc.nc
    with ExitStack() as ctx:
        sb = ctx.enter_context(tc.tile_pool(name="sb", bufs=1))
        ps = ctx.enter_context(tc.psum_pool(name="ps", bufs=1))

        def new(name, width, dtype, tag=""):
            return sb.tile([P, width], dtype, name=name, tag=tag or name, align_bytes=64)

        def load_list(name, src):
            dst = sb.tile([P, J // PER_COLUMN], U16, name=name)
            nc.sync.dma_start(dst[:], src)
            return dst

        def load_words(name, src, width, dtype, tag=""):
            dst = new(name, width, dtype, tag)
            nc.sync.dma_start(dst[:].bitcast(I32), src.bitcast(I32))
            return dst

        def fp8_words(src):
            return src[0].rearrange("p c r -> p (c r)")

        def zeroed_plane(name, width):
            plane = new(name, width, U8)
            nc.gpsimd.memset(plane[:].bitcast(I32), 0)
            return plane

        def load_plane(plane, src):
            for q in range(P // QUADRANT):
                nc.sync.dma_start(
                    plane[QUADRANT * q : QUADRANT * q + 4, :].bitcast(I32),
                    src[0, 4 * q : 4 * q + 4, :].bitcast(I32),
                )

        def deal(copy, walk, name, src, dtype):
            dst = new(name, R, dtype)
            copy(
                dst[:].rearrange("p (t m) -> p " + walk, t=PACK),
                src[:].rearrange("p (m t) -> p " + walk, t=PACK),
            )
            return dst

        def gather_packed(name, table, entries, dtype, tag=""):
            dst = new(name, J, dtype, tag)
            nc.vector.tensor_copy(dst[:], table[:].indirect(entries[:]))
            return dst

        def first_stage(sums, order, weights, weight_scales, weight_fmt, picked, picked_scales, picked_fmt):
            for t in order:
                cols = slice(t * P, (t + 1) * P)
                nc.tensor.matmul_mx(
                    sums[t], lhsT=weights[:, cols].bitcast(weight_fmt), lhsT_scale=weight_scales[:, cols],
                    rhs=picked[:].bitcast(picked_fmt), rhs_scale=picked_scales[:], start=True, stop=True,
                )

        def on_vector(dst, src):
            nc.vector.tensor_copy(dst, src)

        def on_scalar(dst, src):
            nc.scalar.activation(dst, src, ACT.Copy)

        def leave_psum(move, name, src, width, tag=""):
            vals = new(name, width, F32, tag)
            move(vals[:], src)
            return vals

        xt_plane = zeroed_plane("xt_plane", T)
        w_plane = zeroed_plane("w_plane", R)
        xo_plane = zeroed_plane("xo_plane", Z)
        w2_plane = zeroed_plane("w2_plane", R)
        second_planes = zeroed_plane("second_planes", 2 * N + O)
        wb_plane, ws_plane, sx_plane = second_planes[:, :N], second_planes[:, N : 2 * N], second_planes[:, 2 * N :]

        warm_in = new("warm_in", 1, F32)
        warm_out = new("warm_out", 1, F32)
        nc.vector.memset(warm_in[:], 0.0)
        nc.scalar.activation(warm_out[:], warm_in[:], ACT.Sigmoid)

        idx = load_list("idx", offs)
        xt_w = load_words("xt_w", xt_words[0], T, U16)
        load_plane(xt_plane, xt_scales)
        w_w = load_words("w_w", fp8_words(w_words), R, U32)
        load_plane(w_plane, w_scales)
        idx3 = load_list("idx3", offs3)
        idx2 = load_list("idx2", offs2)
        xo_w = load_words("xo_w", fp8_words(xo_words), Z, U32)
        w2_w = load_words("w2_w", fp8_words(w2_words), R, U32)
        load_plane(xo_plane, xo_scales)
        load_plane(w2_plane, w2_scales)
        idx4 = load_list("idx4", offs4)
        idx5 = load_list("idx5", offs5)

        pw = [new("pw%d" % t, C, F32) for t in range(PACK)]
        pv = {t: new("pv%d" % t, C, F32) for t in (0, 2)}
        hid = sb.tile([P, PACK, O], BF16, name="hid", align_bytes=64)

        def add_boards(engine, t):
            whole = new("pg%d" % t, C, F32)
            engine.tensor_tensor(whole[:], pw[t][:], pv[t][:], ALU.add)
            return whole

        xt_g = gather_packed("xt_g", xt_w, idx, U16)
        w_dealt = deal(nc.scalar.copy, "m t", "w_dealt", w_w, U32)
        xt_gs = gather_packed("xt_gs", xt_plane, idx, U8)
        w_dealt_s = deal(nc.vector.tensor_copy, "m t", "w_dealt_s", w_plane, U8)
        a = [ps.tile([P, J], F32, name="a%d" % t) for t in range(PACK)]
        first_stage([bank[:] for bank in a], (1, 0, 2, 3), w_dealt, w_dealt_s, E5M2, xt_g, xt_gs, E2M1)

        for t in range(PACK):
            nc.vector.memset(pw[t][:].bitcast(I32), 0)
        for t in (0, 2):
            nc.vector.memset(pv[t][:].bitcast(I32), 0)

        ws_w = load_words("ws_w", fp8_words(ws_words), N, U32, "xt_w")
        sx_w = load_words("sx_w", fp8_words(sx_words), O, U32, "w_w")
        wb_w = load_words("wb_w", fp8_words(wb_words), N, U32, "xt_plane")
        load_plane(ws_plane, ws_scales)
        load_plane(sx_plane, sx_scales)
        load_plane(wb_plane, wb_scales)
        idx6 = load_list("idx6", offs6)

        a0s = leave_psum(on_scalar, "a0s", a[0][:], J)
        a2s = leave_psum(on_scalar, "a2s", a[2][:], J)
        on_scalar(pw[0][:].indirect(idx3[:]), a0s[:])
        a1s = leave_psum(on_vector, "a1s", a[1][:], J)
        on_vector(pw[1][:].indirect(idx3[:]), a1s[:])
        w2_dealt = deal(nc.gpsimd.tensor_copy, "t m", "w2_dealt", w2_w, U32)
        xo_g = gather_packed("xo_g", xo_w, idx2, U32, "a1s")
        xo_gs = gather_packed("xo_gs", xo_plane, idx2, U8, "xt_gs")
        w2_dealt_s = deal(nc.gpsimd.tensor_copy, "t m", "w2_dealt_s", w2_plane, U8)
        for t, tag in ((1, "w2_w"), (3, "w2_plane")):
            pv[t] = new("pv%d" % t, C, F32, tag)
            nc.gpsimd.memset(pv[t][:].bitcast(I32), 0)
        b01 = ps.tile([P, 2 * J], F32, name="b01", tag="b01")
        b23 = ps.tile([P, 2 * J], F32, name="b23", tag="b23")
        b = [b01[:, :J], b01[:, J:], b23[:, :J], b23[:, J:]]
        first_stage(b, range(PACK), w2_dealt, w2_dealt_s, E4M3, xo_g, xo_gs, E5M2)
        on_scalar(pw[2][:].indirect(idx3[:]), a2s[:])
        a3s = leave_psum(on_vector, "a3s", a[3][:], J, "xo_plane")
        on_vector(pw[3][:].indirect(idx3[:]), a3s[:])

        tz_rows = []
        for h, tag in enumerate(("xo_w", "w_dealt")):
            table = new("tz%d" % h, E, F32, tag)
            nc.sync.dma_start(table[:], tz[h * P : (h + 1) * P, :])
            tz_rows.append(table)
        slope = new("slope", ROW_TILES, F32, "w_plane")
        offset = new("offset", ROW_TILES, F32, "w_dealt_s")
        with nc.allow_non_contiguous_dma(reason="one value a partition for each tile of output features"):
            nc.sync.dma_start(slope[:], so.rearrange("(h p) o -> p (h o)", p=P))
            nc.sync.dma_start(offset[:], bo.rearrange("(h p) o -> p (h o)", p=P))

        b01s = leave_psum(on_scalar, "b01s", b01[:], 2 * J)
        b23s = leave_psum(on_scalar, "b23s", b23[:], 2 * J)

        parts = [slice(i * P, (i + 1) * P) for i in range(PARTS)]
        acc = [ps.tile([P, ROW_TILES, P], F32, name="acc%d" % i, tag=tag) for i, tag in enumerate(("b01", "b23"))]
        for i, cols in enumerate(parts):
            for h in range(ROW_TILES):
                rows = slice(h * P, (h + 1) * P)
                nc.tensor.matmul_mx(
                    acc[i][:, h, :], lhsT=ws_w[:, rows].bitcast(E4M3), lhsT_scale=ws_plane[:, rows],
                    rhs=sx_w[:, cols].bitcast(E5M2), rhs_scale=sx_plane[:, cols], start=(h == 0), stop=False,
                )

        half = J // 2
        on_scalar(pv[0][:].indirect(idx4[:]), b01s[:, :J])
        on_vector(pv[2][:].indirect(idx4[:]), b23s[:, :J])
        on_scalar(pv[1][:].indirect(idx4[:]), b01s[:, J:])
        on_vector(pv[3][:].indirect(idx4[:, : half // PER_COLUMN]), b23s[:, J : J + half])
        on_scalar(pv[3][:].indirect(idx4[:, half // PER_COLUMN :]), b23s[:, J + half :])
        pg = {0: add_boards(nc.gpsimd, 0)}
        for t in (2, 1, 3):
            pg[t] = add_boards(nc.vector, t)

        for t in (0, 2):
            on_scalar(hid[:, t, :], pg[t][:].indirect(idx5[:]))
        for cols in parts:
            entries = idx5[:, cols.start // PER_COLUMN : cols.stop // PER_COLUMN]
            on_scalar(hid[:, 1, cols], pg[1][:].indirect(entries))
            on_vector(hid[:, 3, cols], pg[3][:].indirect(entries))

        gate = sb.tile([P, ROW_TILES, O], F32, name="gate", align_bytes=64)
        for h in range(ROW_TILES):
            nc.scalar.activation(
                gate[:, h, :], tz_rows[h][:].indirect(idx6[:]), ACT.Sigmoid,
                bias=offset[:, h : h + 1], scale=slope[:, h : h + 1],
            )

        woven = [new("woven%d" % i, PACK * P, BF16) for i in range(PARTS)]
        for i, cols in enumerate(parts):
            nc.vector.tensor_copy(
                woven[i][:].rearrange("p (c n t) -> p c t n", n=RUN, t=PACK),
                hid[:, :, cols].rearrange("p t (c n) -> p c t n", n=RUN),
            )
        for i in range(PARTS):
            hid_codes = new("hid_codes%d" % i, P, U32)
            hid_plane = new("hid_plane%d" % i, P, U8)
            nc.vector.quantize_mx(hid_codes[:].bitcast(E5M2), hid_plane[:], woven[i][:])
            for h in range(ROW_TILES):
                rows = slice(h * P, (h + 1) * P)
                nc.tensor.matmul_mx(
                    acc[i][:, h, :], lhsT=wb_w[:, rows].bitcast(E4M3), lhsT_scale=wb_plane[:, rows],
                    rhs=hid_codes[:].bitcast(E5M2), rhs_scale=hid_plane[:], start=False, stop=(h == ROW_TILES - 1),
                )

        out_rows = out.rearrange("(h p) o -> p h o", p=P)
        for i, cols in enumerate(parts):
            y = sb.tile([P, ROW_TILES, P], F32, name="y%d" % i, align_bytes=64)
            nc.vector.tensor_tensor(y[:], acc[i][:], gate[:, :, cols], ALU.mult)
            nc.sync.dma_start(out_rows[:, :, cols], y[:])
